import numpy as np
import ml_dtypes


def mxq(x, axis, fmt="e4m3"):
    dtype, down = {"e4m3": (ml_dtypes.float8_e4m3fn, 7), "e5m2": (ml_dtypes.float8_e5m2, 14)}[fmt]
    v = np.moveaxis(np.asarray(x, np.float32).astype(ml_dtypes.bfloat16).astype(np.float64), axis, -1)
    blocks = v.reshape(v.shape[:-1] + (-1, 32))
    amax = np.abs(blocks).max(-1, keepdims=True)
    byte = np.maximum(np.where(amax > 0, np.frexp(amax)[1] - 1 + 127, 0) - down, 1)
    scale = np.exp2(byte - 127.0)
    codes = (blocks / scale).astype(np.float32).astype(dtype).astype(np.float64)
    return np.moveaxis((codes * scale).reshape(v.shape), -1, axis)


WIDE = False


def mx_kscale(k):
    if not WIDE:
        return np.ones(k)
    levels = np.array([10, -10, 5, -5, 0])
    if k % 512:
        return np.exp2(np.random.permutation(np.resize(levels, k // 32))).repeat(32)
    a = np.empty((k // 512, 16))
    for p in range(k // 512):
        a[p, :8] = np.random.permutation(np.resize(levels, 8))
        for g in range(8):
            far = levels[np.abs(levels - a[p, g]) >= 10]
            a[p, g + 8] = far[np.random.randint(len(far))]
    return np.exp2(a.ravel()).repeat(32)


def f64(x):
    return np.asarray(x).astype(np.float64)


def striped(idx):
    return np.tile(np.asarray(idx).reshape(-1, 16).T, (8, 1)).astype(np.uint16)


def unstriped(offs):
    return offs[:16].T.reshape(-1).astype(np.int64)


E2M1 = np.array([0.0, 0.5, 1.0, 1.5, 2.0, 3.0, 4.0, 6.0, -0.0, -0.5, -1.0, -1.5, -2.0, -3.0, -4.0, -6.0])


def pack_weight(w, fmt):
    k, n = w.shape
    w = f64(np.asarray(w, np.float32).astype(ml_dtypes.bfloat16)).reshape(k // 32, 32, n)
    amax = np.abs(w).max(1)
    if fmt == "e4m3":
        byte = np.frexp(amax)[1] - 1 + 127 - 7
    else:
        mant, ex = np.frexp(amax / 6.0)
        byte = np.where(mant > 0.5, ex, ex - 1) + 127
    byte = np.clip(np.where(amax > 0, byte, 1), 1, 254)
    scaled = (w * np.exp2(127.0 - byte)[:, None, :]).reshape(k, n).astype(np.float32)
    by_word = np.ascontiguousarray(scaled.reshape(k // 512, 128, 4, n).transpose(0, 1, 3, 2))
    if fmt == "e4m3":
        words = by_word.astype(ml_dtypes.float8_e4m3fn).view(np.uint8)
    else:
        c = by_word.astype(ml_dtypes.float4_e2m1fn).view(np.uint8) & 0xF
        words = (c[..., 0::2] | (c[..., 1::2] << 4)).reshape(k // 512, 128, 2 * n)
    return np.ascontiguousarray(words), np.ascontiguousarray(byte.astype(np.uint8).reshape(k // 512, 16, n))


def unpack_weight(words, scales, fmt):
    g, _, n = scales.shape
    words = np.ascontiguousarray(words).reshape(g, 128, n, -1)
    if fmt == "e4m3":
        vals = words.view(ml_dtypes.float8_e4m3fn).astype(np.float64)
    else:
        nib = np.empty((g, 128, n, 4), np.uint8)
        nib[..., 0::2] = words & 0xF
        nib[..., 1::2] = words >> 4
        vals = E2M1[nib]
    vals = vals * np.repeat(np.exp2(scales.astype(np.float64) - 127.0), 8, axis=1)[..., None]
    return vals.transpose(0, 1, 3, 2).reshape(g * 512, n)


def bf(x):
    return np.asarray(x, np.float32).astype(ml_dtypes.bfloat16)


def planes(Y):
    r, m = Y.shape
    b = f64(bf(Y)).reshape(r // 32, 32, m)
    amax = np.abs(b).max(1)
    byte = np.clip(np.where(amax > 0, np.frexp(amax)[1] - 1 + 127 - 7, 1), 1, 254)
    codes = (b * np.exp2(127.0 - byte)[:, None, :]).reshape(r, m).astype(np.float32).astype(ml_dtypes.float8_e4m3fn).view(np.uint8)
    words = codes.reshape(r // 512, 128, 4, m).transpose(0, 1, 3, 2)
    return np.ascontiguousarray(words), np.ascontiguousarray(byte.astype(np.uint8).reshape(r // 512, 16, m))


D, T, I, J, U, Z, M = 512, 2048, 512, 512, 1024, 1024, 1024


def setup_inputs():
    n = np.random.standard_normal
    idx = np.random.permutation(T)[:I]
    idx2 = np.random.permutation(U)[:J]
    idx3 = np.random.permutation(Z)[:J]
    idx4 = np.random.permutation(M)[:J]
    fd = mx_kscale(D)
    keysp = pack_weight(n((D, T)) / fd[:, None], "e2m1")
    return {
        "keys_words": keysp[0],
        "keys_scales": keysp[1],
        "notes": (n((D, U)) * 1.0 / np.sqrt(D) * fd[:, None]).astype(np.float32),
        "given": (np.random.uniform(0.3, 1.7, (I, Z))).astype(np.float32),
        "old": (1.0 * n((I, M))).astype(np.float32),
        "fade": (np.random.uniform(0.3, 0.9, (I, 1))).astype(np.float32),
        "offs": striped(idx),
        "offs2": striped(idx2),
        "offs3": striped(idx3),
        "offs4": striped(idx4),
    }


def reference(keys_words, keys_scales, notes, given, old, fade, offs, offs2, offs3, offs4):
    idx = unstriped(offs)
    idx2 = unstriped(offs2)
    idx3 = unstriped(offs3)
    idx4 = unstriped(offs4)
    keysu = unpack_weight(keys_words, keys_scales, "e2m1")
    keysidxg = keysu[:, idx]
    notesidx2q = mxq(f64(notes)[:, idx2], 0, "e4m3")
    g1 = keysidxg.T @ notesidx2q
    g0 = g1 * f64(given)[:, idx3]
    gf = np.zeros((I, M))
    gf[:, idx4] = g0
    y = f64(old) * f64(fade) + gf
    words, scales = planes(y)
    return y, words, scales

@@ -1,0 +1,195 @@
+from contextlib import ExitStack
+
+import concourse.mybir as mybir
+
+D, T, I, J, U, Z, M = 512, 2048, 512, 512, 1024, 1024, 1024
+FLOPS = 2 * D * I * J
+
+F32 = mybir.dt.float32
+BF16 = mybir.dt.bfloat16
+I32 = mybir.dt.int32
+U32 = mybir.dt.uint32
+U16 = mybir.dt.uint16
+U8 = mybir.dt.uint8
+FP8X4 = mybir.dt.float8_e4m3fn_x4
+FP4X4 = mybir.dt.float4_e2m1fn_x4
+MULT = mybir.AluOpType.mult
+ADD = mybir.AluOpType.add
+COPY = mybir.ActivationFunctionType.Copy
+
+P = 128
+PACK = 4
+LIST_COLS = J // 16
+HALF = J // 2
+CHUNKS = 4
+CHUNK = M // CHUNKS
+
+
+def tile_attend_tab_timestable_keep_pl_kernel(
+    tc, keys_words, keys_scales, notes, given, old, fade, offs, offs2, offs3, offs4, out_0, out_1, out_2
+):
+    nc = tc.nc
+    with ExitStack() as ctx:
+        sb = ctx.enter_context(tc.tile_pool(name="sb", bufs=1))
+        ps = ctx.enter_context(tc.psum_pool(name="ps", bufs=1))
+
+        def listed(name, src):
+            tile = sb.tile([P, LIST_COLS], U16, name=name)
+            nc.sync.dma_start(tile[:], src)
+            return tile
+
+        def half(lst, h):
+            return lst[:, h * LIST_COLS // 2 : (h + 1) * LIST_COLS // 2]
+
+        notes_rows = notes.rearrange("(p t) u -> p t u", t=PACK)
+        given_rows = given.rearrange("(p t) z -> p t z", t=PACK)
+        old_rows = old.rearrange("(p t) m -> p t m", t=PACK)
+        out_rows = out_0.rearrange("(p t) m -> p t m", t=PACK)
+
+        key_scales = sb.tile([P, T], U8, name="key_scales")
+        nc.vector.memset(key_scales[:].bitcast(I32), 0)
+        for q in range(4):
+            nc.sync.dma_start(
+                key_scales[32 * q : 32 * q + 4, :].bitcast(I32), keys_scales[0, 4 * q : 4 * q + 4, :].bitcast(I32)
+            )
+
+        note_planes = [sb.tile([P, U], F32, name="note_plane%d" % t) for t in range(PACK)]
+        nc.sync.dma_start(note_planes[0][:], notes_rows[:, 0, :])
+        note_list = listed("note_list", offs2)
+        key_words = sb.tile([P, T], U16, name="key_words")
+        nc.sync.dma_start(key_words[:].bitcast(I32), keys_words[0].bitcast(I32))
+        token_list = listed("token_list", offs)
+        for t in range(1, PACK):
+            nc.sync.dma_start(note_planes[t][:], notes_rows[:, t, :])
+        given_list = listed("given_list", offs3)
+        given_lo = [sb.tile([P, Z], F32, name="given%d" % t) for t in range(2)]
+        given_hi = sb.tile([P, 2, Z], F32, name="given_hi")
+        olds = [sb.tile([P, M], F32, name="old%d" % t) for t in range(PACK)]
+        for t in range(2):
+            nc.sync.dma_start(given_lo[t][:], given_rows[:, t, :])
+        place_list = listed("place_list", offs4)
+        fades = sb.tile([P, PACK], F32, name="fades")
+        nc.sync.dma_start(fades[:], fade.rearrange("(p t) o -> p (t o)", t=PACK))
+        nc.sync.dma_start(olds[0][:], old_rows[:, 0, :])
+        nc.sync.dma_start(given_hi[:], given_rows[:, 2:4, :])
+        for t in range(1, PACK):
+            nc.sync.dma_start(olds[t][:], old_rows[:, t, :])
+        givens = [given_lo[0][:], given_lo[1][:], given_hi[:, 0, :], given_hi[:, 1, :]]
+
+        windows = [sb.tile([P, M], F32, name="window%d" % w) for w in range(2)]
+        for window in windows:
+            nc.vector.memset(window[:], 0.0)
+        placed = [windows[t % 2] for t in range(PACK)]
+
+        picked_words = sb.tile([P, I], U16, name="picked_words")
+        nc.vector.tensor_copy(picked_words[:], key_words[:].indirect(token_list[:]))
+        dealt_words = sb.tile([P, PACK, P], U16, name="dealt_words", align_bytes=64)
+        nc.vector.tensor_copy(dealt_words[:], picked_words[:].rearrange("p (s t) -> p t s", t=PACK))
+        dealt_scales = sb.tile([P, PACK, P], U8, name="dealt_scales", align_bytes=64)
+        nc.vector.tensor_copy(dealt_scales[:].rearrange("p t s -> p s t"), key_scales[:].indirect(token_list[:]))
+
+        picked_notes = sb.tile([P, PACK, J], F32, name="picked_notes")
+        for t in range(2):
+            nc.scalar.activation(picked_notes[:, t, :], note_planes[t][:].indirect(note_list[:]), COPY)
+        nc.vector.tensor_copy(picked_notes[:, 2, :], note_planes[2][:].indirect(note_list[:]))
+        last = PACK - 1
+        nc.vector.tensor_copy(picked_notes[:, last, 0:HALF], note_planes[last][:].indirect(half(note_list, 0)))
+        nc.scalar.activation(picked_notes[:, last, HALF:J], note_planes[last][:].indirect(half(note_list, 1)), COPY)
+        woven_notes = sb.tile([P, J, PACK], BF16, name="woven_notes", align_bytes=64)
+        note_codes = sb.tile([P, J], U32, name="note_codes", align_bytes=64)
+        note_scales = sb.tile([P, J], U8, name="note_scales", align_bytes=64)
+        halves = [slice(h * HALF, (h + 1) * HALF) for h in range(2)]
+        for cols in halves:
+            nc.vector.tensor_copy(woven_notes[:, cols, :], picked_notes[:, :, cols].rearrange("p t j -> p j t"))
+        for cols in halves:
+            nc.vector.quantize_mx(
+                out=note_codes[:, cols].bitcast(FP8X4),
+                scales=note_scales[:, cols],
+                in_=woven_notes[:, cols, :].rearrange("p j t -> p (j t)"),
+            )
+
+        banks = [ps.tile([P, J], F32, name="bank%d" % t) for t in range(PACK)]
+        for t in range(PACK):
+            for cols in halves:
+                nc.tensor.matmul_mx(
+                    out=banks[t][:, cols],
+                    lhsT=dealt_words[:, t, :].bitcast(FP4X4),
+                    lhsT_scale=dealt_scales[:, t, :],
+                    rhs=note_codes[:, cols].bitcast(FP8X4),
+                    rhs_scale=note_scales[:, cols],
+                    start=True,
+                    stop=True,
+                )
+
+        picked_given = [sb.tile([P, J], F32, name="picked_given%d" % t) for t in range(PACK)]
+        table = [sb.tile([P, J], F32, name="table%d" % t) for t in range(PACK)]
+        result = sb.tile([P, PACK, M], F32, name="result")
+        parked = result[:, 2, 0:HALF]
+
+        def pick_given(t):
+            nc.scalar.activation(picked_given[t][:], givens[t].indirect(given_list[:]), COPY)
+
+        def scale(t):
+            nc.vector.tensor_tensor(table[t][:], banks[t][:], picked_given[t][:], MULT)
+
+        def place_on_scalar(t, h):
+            nc.scalar.activation(placed[t][:].indirect(half(place_list, h)), table[t][:, halves[h]], COPY)
+
+        def add_old(t, cols):
+            nc.vector.scalar_tensor_tensor(
+                result[:, t, cols], olds[t][:, cols], fades[:, t : t + 1], placed[t][:, cols], MULT, ADD
+            )
+
+        def store_rows(t):
+            nc.sync.dma_start(out_rows[:, t, :], result[:, t, :])
+
+        whole = slice(0, M)
+        pick_given(0)
+        pick_given(1)
+        scale(0)
+        scale(1)
+        place_on_scalar(0, 0)
+        place_on_scalar(0, 1)
+        nc.vector.tensor_copy(placed[1][:].indirect(place_list[:]), table[1][:])
+        add_old(0, whole)
+        store_rows(0)
+        pick_given(2)
+        pick_given(3)
+        scale(2)
+        nc.vector.tensor_tensor(parked, banks[3][:, halves[0]], picked_given[3][:, halves[0]], MULT)
+        nc.vector.tensor_tensor(table[3][:, halves[1]], banks[3][:, halves[1]], picked_given[3][:, halves[1]], MULT)
+        place_on_scalar(2, 0)
+        place_on_scalar(2, 1)
+        add_old(1, whole)
+        store_rows(1)
+        nc.vector.tensor_copy(placed[3][:].indirect(half(place_list, 0)), parked)
+        place_on_scalar(3, 1)
+        add_old(2, whole)
+        store_rows(2)
+        chunks = [slice(c * CHUNK, (c + 1) * CHUNK) for c in range(CHUNKS)]
+        for cols in chunks:
+            add_old(3, cols)
+        store_rows(3)
+
+        woven = [sb.tile([P, CHUNK, PACK], BF16, name="woven%d" % c, align_bytes=64) for c in range(CHUNKS)]
+        codes = sb.tile([P, M], U32, name="codes", align_bytes=64)
+        scales = sb.tile([P, M], U8, name="scales", align_bytes=64)
+        for c in range(CHUNKS):
+            src = result[:, :, chunks[c]].rearrange("p t m -> p m t")
+            if c < CHUNKS // 2:
+                nc.scalar.copy(woven[c][:], src)
+            else:
+                nc.vector.tensor_copy(woven[c][:], src)
+        words_out = out_1[0].rearrange("p m t -> p (m t)").bitcast(I32)
+        for c in (0, 2, 3, 1):
+            nc.vector.quantize_mx(
+                out=codes[:, chunks[c]].bitcast(FP8X4),
+                scales=scales[:, chunks[c]],
+                in_=woven[c][:].rearrange("p m t -> p (m t)"),
+            )
+            nc.sync.dma_start(words_out[:, chunks[c]], codes[:, chunks[c]].bitcast(I32))
+        for q in range(4):
+            queue = nc.sync if q % 2 else nc.scalar
+            queue.dma_start(
+                out_2[0, 4 * q : 4 * q + 4, :].bitcast(I32), scales[32 * q : 32 * q + 4, :].bitcast(I32)
+            )

@@ -21,6 +21,7 @@ P = 128
 PACK = 4
 LIST_COLS = J // 16
 HALF = J // 2
+VECTOR_SHARE = 320
 CHUNKS = 4
 CHUNK = M // CHUNKS
 
@@ -38,8 +39,14 @@ def tile_attend_tab_timestable_keep_pl_kernel(
             nc.sync.dma_start(tile[:], src)
             return tile
 
+        def entries(lst, cols):
+            return lst[:, cols.start // 16 : cols.stop // 16]
+
         def half(lst, h):
-            return lst[:, h * LIST_COLS // 2 : (h + 1) * LIST_COLS // 2]
+            return entries(lst, slice(h * HALF, (h + 1) * HALF))
+
+        def weave(copy, out, in_):
+            copy(out.rearrange("p (c i) t -> p c t i", i=4), in_.rearrange("p t (c i) -> p c t i", i=4))
 
         notes_rows = notes.rearrange("(p t) u -> p t u", t=PACK)
         given_rows = given.rearrange("(p t) z -> p t z", t=PACK)
@@ -89,9 +96,8 @@ def tile_attend_tab_timestable_keep_pl_kernel(
         nc.vector.tensor_copy(dealt_scales[:].rearrange("p t s -> p s t"), key_scales[:].indirect(token_list[:]))
 
         picked_notes = sb.tile([P, PACK, J], F32, name="picked_notes")
-        for t in range(2):
+        for t in range(PACK - 1):
             nc.scalar.activation(picked_notes[:, t, :], note_planes[t][:].indirect(note_list[:]), COPY)
-        nc.vector.tensor_copy(picked_notes[:, 2, :], note_planes[2][:].indirect(note_list[:]))
         last = PACK - 1
         nc.vector.tensor_copy(picked_notes[:, last, 0:HALF], note_planes[last][:].indirect(half(note_list, 0)))
         nc.scalar.activation(picked_notes[:, last, HALF:J], note_planes[last][:].indirect(half(note_list, 1)), COPY)
@@ -99,8 +105,9 @@ def tile_attend_tab_timestable_keep_pl_kernel(
         note_codes = sb.tile([P, J], U32, name="note_codes", align_bytes=64)
         note_scales = sb.tile([P, J], U8, name="note_scales", align_bytes=64)
         halves = [slice(h * HALF, (h + 1) * HALF) for h in range(2)]
+        weave(nc.vector.tensor_copy, woven_notes[:, :, 0:2], picked_notes[:, 0:2, :])
         for cols in halves:
-            nc.vector.tensor_copy(woven_notes[:, cols, :], picked_notes[:, :, cols].rearrange("p t j -> p j t"))
+            weave(nc.vector.tensor_copy, woven_notes[:, cols, 2:4], picked_notes[:, 2:4, cols])
         for cols in halves:
             nc.vector.quantize_mx(
                 out=note_codes[:, cols].bitcast(FP8X4),
@@ -124,7 +131,8 @@ def tile_attend_tab_timestable_keep_pl_kernel(
         picked_given = [sb.tile([P, J], F32, name="picked_given%d" % t) for t in range(PACK)]
         table = [sb.tile([P, J], F32, name="table%d" % t) for t in range(PACK)]
         result = sb.tile([P, PACK, M], F32, name="result")
-        parked = result[:, 2, 0:HALF]
+        parked = result[:, 2, 0:VECTOR_SHARE]
+        head, tail = slice(0, VECTOR_SHARE), slice(VECTOR_SHARE, J)
 
         def pick_given(t):
             nc.scalar.activation(picked_given[t][:], givens[t].indirect(given_list[:]), COPY)
@@ -132,8 +140,8 @@ def tile_attend_tab_timestable_keep_pl_kernel(
         def scale(t):
             nc.vector.tensor_tensor(table[t][:], banks[t][:], picked_given[t][:], MULT)
 
-        def place_on_scalar(t, h):
-            nc.scalar.activation(placed[t][:].indirect(half(place_list, h)), table[t][:, halves[h]], COPY)
+        def place_on_scalar(t, cols):
+            nc.scalar.activation(placed[t][:].indirect(entries(place_list, cols)), table[t][:, cols], COPY)
 
         def add_old(t, cols):
             nc.vector.scalar_tensor_tensor(
@@ -148,22 +156,22 @@ def tile_attend_tab_timestable_keep_pl_kernel(
         pick_given(1)
         scale(0)
         scale(1)
-        place_on_scalar(0, 0)
-        place_on_scalar(0, 1)
+        place_on_scalar(0, halves[0])
+        place_on_scalar(0, halves[1])
         nc.vector.tensor_copy(placed[1][:].indirect(place_list[:]), table[1][:])
         add_old(0, whole)
         store_rows(0)
         pick_given(2)
         pick_given(3)
         scale(2)
-        nc.vector.tensor_tensor(parked, banks[3][:, halves[0]], picked_given[3][:, halves[0]], MULT)
-        nc.vector.tensor_tensor(table[3][:, halves[1]], banks[3][:, halves[1]], picked_given[3][:, halves[1]], MULT)
-        place_on_scalar(2, 0)
-        place_on_scalar(2, 1)
+        nc.vector.tensor_tensor(parked, banks[3][:, head], picked_given[3][:, head], MULT)
+        nc.vector.tensor_tensor(table[3][:, tail], banks[3][:, tail], picked_given[3][:, tail], MULT)
+        place_on_scalar(2, halves[0])
+        place_on_scalar(2, halves[1])
         add_old(1, whole)
         store_rows(1)
-        nc.vector.tensor_copy(placed[3][:].indirect(half(place_list, 0)), parked)
-        place_on_scalar(3, 1)
+        nc.vector.tensor_copy(placed[3][:].indirect(entries(place_list, head)), parked)
+        place_on_scalar(3, tail)
         add_old(2, whole)
         store_rows(2)
         chunks = [slice(c * CHUNK, (c + 1) * CHUNK) for c in range(CHUNKS)]
@@ -175,11 +183,8 @@ def tile_attend_tab_timestable_keep_pl_kernel(
         codes = sb.tile([P, M], U32, name="codes", align_bytes=64)
         scales = sb.tile([P, M], U8, name="scales", align_bytes=64)
         for c in range(CHUNKS):
-            src = result[:, :, chunks[c]].rearrange("p t m -> p m t")
-            if c < CHUNKS // 2:
-                nc.scalar.copy(woven[c][:], src)
-            else:
-                nc.vector.tensor_copy(woven[c][:], src)
+            copy = nc.scalar.copy if c < CHUNKS // 2 else nc.vector.tensor_copy
+            weave(copy, woven[c][:], result[:, :, chunks[c]])
         words_out = out_1[0].rearrange("p m t -> p (m t)").bitcast(I32)
         for c in (0, 2, 3, 1):
             nc.vector.quantize_mx(

@@ -53,6 +53,11 @@ def tile_attend_tab_timestable_keep_pl_kernel(
         old_rows = old.rearrange("(p t) m -> p t m", t=PACK)
         out_rows = out_0.rearrange("(p t) m -> p t m", t=PACK)
 
+        warm_in = sb.tile([P, 1], F32, name="warm_in")
+        warm_out = sb.tile([P, 1], F32, name="warm_out")
+        nc.gpsimd.memset(warm_in[:], 0.0)
+        nc.scalar.activation(warm_out[:], warm_in[:], COPY)
+
         key_scales = sb.tile([P, T], U8, name="key_scales")
         nc.vector.memset(key_scales[:].bitcast(I32), 0)
         for q in range(4):

@@ -22,8 +22,6 @@ PACK = 4
 LIST_COLS = J // 16
 HALF = J // 2
 VECTOR_SHARE = 320
-CHUNKS = 4
-CHUNK = M // CHUNKS
 
 
 def tile_attend_tab_timestable_keep_pl_kernel(
@@ -60,17 +58,16 @@ def tile_attend_tab_timestable_keep_pl_kernel(
 
         key_scales = sb.tile([P, T], U8, name="key_scales")
         nc.vector.memset(key_scales[:].bitcast(I32), 0)
+        token_list = listed("token_list", offs)
+        key_words = sb.tile([P, T], U16, name="key_words")
+        nc.sync.dma_start(key_words[:].bitcast(I32), keys_words[0].bitcast(I32))
+        note_planes = [sb.tile([P, U], F32, name="note_plane%d" % t) for t in range(PACK)]
+        nc.sync.dma_start(note_planes[0][:], notes_rows[:, 0, :])
+        note_list = listed("note_list", offs2)
         for q in range(4):
             nc.sync.dma_start(
                 key_scales[32 * q : 32 * q + 4, :].bitcast(I32), keys_scales[0, 4 * q : 4 * q + 4, :].bitcast(I32)
             )
-
-        note_planes = [sb.tile([P, U], F32, name="note_plane%d" % t) for t in range(PACK)]
-        nc.sync.dma_start(note_planes[0][:], notes_rows[:, 0, :])
-        note_list = listed("note_list", offs2)
-        key_words = sb.tile([P, T], U16, name="key_words")
-        nc.sync.dma_start(key_words[:].bitcast(I32), keys_words[0].bitcast(I32))
-        token_list = listed("token_list", offs)
         for t in range(1, PACK):
             nc.sync.dma_start(note_planes[t][:], notes_rows[:, t, :])
         given_list = listed("given_list", offs3)
@@ -179,19 +176,21 @@ def tile_attend_tab_timestable_keep_pl_kernel(
         place_on_scalar(3, tail)
         add_old(2, whole)
         store_rows(2)
-        chunks = [slice(c * CHUNK, (c + 1) * CHUNK) for c in range(CHUNKS)]
+        chunks = [slice(0, M // 4), slice(M // 4, M // 2), slice(M // 2, M)]
         for cols in chunks:
             add_old(3, cols)
         store_rows(3)
 
-        woven = [sb.tile([P, CHUNK, PACK], BF16, name="woven%d" % c, align_bytes=64) for c in range(CHUNKS)]
+        woven = [
+            sb.tile([P, cols.stop - cols.start, PACK], BF16, name="woven%d" % c, align_bytes=64)
+            for c, cols in enumerate(chunks)
+        ]
         codes = sb.tile([P, M], U32, name="codes", align_bytes=64)
         scales = sb.tile([P, M], U8, name="scales", align_bytes=64)
-        for c in range(CHUNKS):
-            copy = nc.scalar.copy if c < CHUNKS // 2 else nc.vector.tensor_copy
+        for c, copy in enumerate((nc.scalar.copy, nc.scalar.copy, nc.vector.tensor_copy)):
             weave(copy, woven[c][:], result[:, :, chunks[c]])
         words_out = out_1[0].rearrange("p m t -> p (m t)").bitcast(I32)
-        for c in (0, 2, 3, 1):
+        for c in (0, 2, 1):
             nc.vector.quantize_mx(
                 out=codes[:, chunks[c]].bitcast(FP8X4),
                 scales=scales[:, chunks[c]],

from contextlib import ExitStack

import concourse.mybir as mybir

D, T, I, J, U, Z, M = 512, 2048, 512, 512, 1024, 1024, 1024
FLOPS = 2 * D * I * J

F32 = mybir.dt.float32
BF16 = mybir.dt.bfloat16
I32 = mybir.dt.int32
U32 = mybir.dt.uint32
U16 = mybir.dt.uint16
U8 = mybir.dt.uint8
FP8X4 = mybir.dt.float8_e4m3fn_x4
FP4X4 = mybir.dt.float4_e2m1fn_x4
MULT = mybir.AluOpType.mult
ADD = mybir.AluOpType.add
COPY = mybir.ActivationFunctionType.Copy

P = 128
PACK = 4
LIST_COLS = J // 16
HALF = J // 2
VECTOR_SHARE = 320


def tile_attend_tab_timestable_keep_pl_kernel(
    tc, keys_words, keys_scales, notes, given, old, fade, offs, offs2, offs3, offs4, out_0, out_1, out_2
):
    nc = tc.nc
    with ExitStack() as ctx:
        sb = ctx.enter_context(tc.tile_pool(name="sb", bufs=1))
        ps = ctx.enter_context(tc.psum_pool(name="ps", bufs=1))

        def listed(name, src):
            tile = sb.tile([P, LIST_COLS], U16, name=name)
            nc.sync.dma_start(tile[:], src)
            return tile

        def entries(lst, cols):
            return lst[:, cols.start // 16 : cols.stop // 16]

        def half(lst, h):
            return entries(lst, slice(h * HALF, (h + 1) * HALF))

        def weave(copy, out, in_):
            copy(out.rearrange("p (c i) t -> p c t i", i=4), in_.rearrange("p t (c i) -> p c t i", i=4))

        notes_rows = notes.rearrange("(p t) u -> p t u", t=PACK)
        given_rows = given.rearrange("(p t) z -> p t z", t=PACK)
        old_rows = old.rearrange("(p t) m -> p t m", t=PACK)
        out_rows = out_0.rearrange("(p t) m -> p t m", t=PACK)

        warm_in = sb.tile([P, 1], F32, name="warm_in")
        warm_out = sb.tile([P, 1], F32, name="warm_out")
        nc.gpsimd.memset(warm_in[:], 0.0)
        nc.scalar.activation(warm_out[:], warm_in[:], COPY)

        key_scales = sb.tile([P, T], U8, name="key_scales")
        nc.vector.memset(key_scales[:].bitcast(I32), 0)
        token_list = listed("token_list", offs)
        key_words = sb.tile([P, T], U16, name="key_words")
        nc.sync.dma_start(key_words[:].bitcast(I32), keys_words[0].bitcast(I32))
        note_planes = [sb.tile([P, U], F32, name="note_plane%d" % t) for t in range(PACK)]
        nc.sync.dma_start(note_planes[0][:], notes_rows[:, 0, :])
        note_list = listed("note_list", offs2)
        for q in range(4):
            nc.sync.dma_start(
                key_scales[32 * q : 32 * q + 4, :].bitcast(I32), keys_scales[0, 4 * q : 4 * q + 4, :].bitcast(I32)
            )
        for t in range(1, PACK):
            nc.sync.dma_start(note_planes[t][:], notes_rows[:, t, :])
        given_list = listed("given_list", offs3)
        given_lo = [sb.tile([P, Z], F32, name="given%d" % t) for t in range(2)]
        given_hi = sb.tile([P, 2, Z], F32, name="given_hi")
        olds = [sb.tile([P, M], F32, name="old%d" % t) for t in range(PACK)]
        for t in range(2):
            nc.sync.dma_start(given_lo[t][:], given_rows[:, t, :])
        place_list = listed("place_list", offs4)
        fades = sb.tile([P, PACK], F32, name="fades")
        nc.sync.dma_start(fades[:], fade.rearrange("(p t) o -> p (t o)", t=PACK))
        nc.sync.dma_start(olds[0][:], old_rows[:, 0, :])
        nc.sync.dma_start(given_hi[:], given_rows[:, 2:4, :])
        for t in range(1, PACK):
            nc.sync.dma_start(olds[t][:], old_rows[:, t, :])
        givens = [given_lo[0][:], given_lo[1][:], given_hi[:, 0, :], given_hi[:, 1, :]]

        windows = [sb.tile([P, M], F32, name="window%d" % w) for w in range(2)]
        for window in windows:
            nc.vector.memset(window[:], 0.0)
        placed = [windows[t % 2] for t in range(PACK)]

        picked_words = sb.tile([P, I], U16, name="picked_words")
        nc.vector.tensor_copy(picked_words[:], key_words[:].indirect(token_list[:]))
        dealt_words = sb.tile([P, PACK, P], U16, name="dealt_words", align_bytes=64)
        nc.vector.tensor_copy(dealt_words[:], picked_words[:].rearrange("p (s t) -> p t s", t=PACK))
        dealt_scales = sb.tile([P, PACK, P], U8, name="dealt_scales", align_bytes=64)
        nc.vector.tensor_copy(dealt_scales[:].rearrange("p t s -> p s t"), key_scales[:].indirect(token_list[:]))

        picked_notes = sb.tile([P, PACK, J], F32, name="picked_notes")
        for t in range(PACK - 1):
            nc.scalar.activation(picked_notes[:, t, :], note_planes[t][:].indirect(note_list[:]), COPY)
        last = PACK - 1
        nc.vector.tensor_copy(picked_notes[:, last, 0:HALF], note_planes[last][:].indirect(half(note_list, 0)))
        nc.scalar.activation(picked_notes[:, last, HALF:J], note_planes[last][:].indirect(half(note_list, 1)), COPY)
        woven_notes = sb.tile([P, J, PACK], BF16, name="woven_notes", align_bytes=64)
        note_codes = sb.tile([P, J], U32, name="note_codes", align_bytes=64)
        note_scales = sb.tile([P, J], U8, name="note_scales", align_bytes=64)
        halves = [slice(h * HALF, (h + 1) * HALF) for h in range(2)]
        weave(nc.vector.tensor_copy, woven_notes[:, :, 0:2], picked_notes[:, 0:2, :])
        for cols in halves:
            weave(nc.vector.tensor_copy, woven_notes[:, cols, 2:4], picked_notes[:, 2:4, cols])
        for cols in halves:
            nc.vector.quantize_mx(
                out=note_codes[:, cols].bitcast(FP8X4),
                scales=note_scales[:, cols],
                in_=woven_notes[:, cols, :].rearrange("p j t -> p (j t)"),
            )

        banks = [ps.tile([P, J], F32, name="bank%d" % t) for t in range(PACK)]
        for t in range(PACK):
            for cols in halves:
                nc.tensor.matmul_mx(
                    out=banks[t][:, cols],
                    lhsT=dealt_words[:, t, :].bitcast(FP4X4),
                    lhsT_scale=dealt_scales[:, t, :],
                    rhs=note_codes[:, cols].bitcast(FP8X4),
                    rhs_scale=note_scales[:, cols],
                    start=True,
                    stop=True,
                )

        picked_given = [sb.tile([P, J], F32, name="picked_given%d" % t) for t in range(PACK)]
        table = [sb.tile([P, J], F32, name="table%d" % t) for t in range(PACK)]
        result = sb.tile([P, PACK, M], F32, name="result")
        parked = result[:, 2, 0:VECTOR_SHARE]
        head, tail = slice(0, VECTOR_SHARE), slice(VECTOR_SHARE, J)

        def pick_given(t):
            nc.scalar.activation(picked_given[t][:], givens[t].indirect(given_list[:]), COPY)

        def scale(t):
            nc.vector.tensor_tensor(table[t][:], banks[t][:], picked_given[t][:], MULT)

        def place_on_scalar(t, cols):
            nc.scalar.activation(placed[t][:].indirect(entries(place_list, cols)), table[t][:, cols], COPY)

        def add_old(t, cols):
            nc.vector.scalar_tensor_tensor(
                result[:, t, cols], olds[t][:, cols], fades[:, t : t + 1], placed[t][:, cols], MULT, ADD
            )

        def store_rows(t):
            nc.sync.dma_start(out_rows[:, t, :], result[:, t, :])

        whole = slice(0, M)
        pick_given(0)
        pick_given(1)
        scale(0)
        scale(1)
        place_on_scalar(0, halves[0])
        place_on_scalar(0, halves[1])
        nc.vector.tensor_copy(placed[1][:].indirect(place_list[:]), table[1][:])
        add_old(0, whole)
        store_rows(0)
        pick_given(2)
        pick_given(3)
        scale(2)
        nc.vector.tensor_tensor(parked, banks[3][:, head], picked_given[3][:, head], MULT)
        nc.vector.tensor_tensor(table[3][:, tail], banks[3][:, tail], picked_given[3][:, tail], MULT)
        place_on_scalar(2, halves[0])
        place_on_scalar(2, halves[1])
        add_old(1, whole)
        store_rows(1)
        nc.vector.tensor_copy(placed[3][:].indirect(entries(place_list, head)), parked)
        place_on_scalar(3, tail)
        add_old(2, whole)
        store_rows(2)
        chunks = [slice(0, M // 4), slice(M // 4, M // 2), slice(M // 2, M)]
        for cols in chunks:
            add_old(3, cols)
        store_rows(3)

        woven = [
            sb.tile([P, cols.stop - cols.start, PACK], BF16, name="woven%d" % c, align_bytes=64)
            for c, cols in enumerate(chunks)
        ]
        codes = sb.tile([P, M], U32, name="codes", align_bytes=64)
        scales = sb.tile([P, M], U8, name="scales", align_bytes=64)
        for c, copy in enumerate((nc.scalar.copy, nc.scalar.copy, nc.vector.tensor_copy)):
            weave(copy, woven[c][:], result[:, :, chunks[c]])
        words_out = out_1[0].rearrange("p m t -> p (m t)").bitcast(I32)
        for c in (0, 2, 1):
            nc.vector.quantize_mx(
                out=codes[:, chunks[c]].bitcast(FP8X4),
                scales=scales[:, chunks[c]],
                in_=woven[c][:].rearrange("p m t -> p (m t)"),
            )
            nc.sync.dma_start(words_out[:, chunks[c]], codes[:, chunks[c]].bitcast(I32))
        for q in range(4):
            queue = nc.sync if q % 2 else nc.scalar
            queue.dma_start(
                out_2[0, 4 * q : 4 * q + 4, :].bitcast(I32), scales[32 * q : 32 * q + 4, :].bitcast(I32)
            )
